import numpy as np
CORES = [1,0]
N = 2
def setup_inputs(rng):
    return {"x": rng.standard_normal((N, 128, 4), dtype=np.float32)}
def reference(x):
    s = x.sum(axis=0, dtype=np.float64).astype(x.dtype)
    b = 4 // N
    return {"y": np.stack([s[:, r * b:(r + 1) * b] for r in range(N)])}

from concourse.mybir import AluOpType

SCRATCH = {
    "send": ("sbuf", [128, 2], "float32"),
    "land": ("sbuf", [128, 2], "float32"),
}
SEMAPHORES = ["staged", "seeded", "left", "arrived", "stored"]


def rank_program(g, core, T, topo):
    rank = T.rank_of(core)
    if rank is None:
        return

    n = len(T.cores)
    b = T.x.shape[1] // n
    peer_rank = 1 - rank
    peer = T.cores[peer_rank]
    rid, pid, sengine = topo.addr(peer)
    mask = topo.mask(core, peer)
    engines = bin(mask).count("1")

    g.dma_start(T.send[:], T.x[:, peer_rank * b:(peer_rank + 1) * b]).then_inc(T.sem.staged, 16)
    g.dma_start(T.y[:], T.x[:, rank * b:(rank + 1) * b]).then_inc(T.sem.seeded, 16)

    g.wait_ge(T.sem.staged, 16)
    g.remote_dma(T.land[:], T.send[:], T.sem.arrived, T.sem.left, pid, rid, mask)

    g.wait_ge(T.sem.seeded, 16)
    g.wait_ge(T.sem.arrived, engines)
    g.dma_start(T.y[:], T.land[:], accum_op=AluOpType.add).then_inc(T.sem.stored, 16)

    g.wait_ge(T.sem.left, engines)
    g.wait_ge(T.sem.stored, 16)
